import numpy as np
import ml_dtypes

BF16 = ml_dtypes.bfloat16


def bf(x):
    return np.asarray(x, np.float32).astype(BF16)


def f32(x):
    return np.asarray(x, np.float32)


def f64(x):
    return np.asarray(x).astype(np.float64)


def striped(idx):
    return np.tile(idx.reshape(-1, 16).T, (8, 1))


S, K, M, N, D, V = 512, 128, 512, 192, 2, 96


def setup_inputs():
    return {"table": bf(np.random.standard_normal((K, S))), "w": bf(np.random.standard_normal((K, M)) / np.sqrt(D * K)), "c": f32(0.2 + 0.8 * np.random.random_sample((1, V))), "offs": striped(np.random.permutation(np.tile(np.arange(S), 2))[:N])}


def reference(table, w, c, offs):
    idx = offs[:16].T.reshape(-1)
    x = f64(table)[:, idx]
    y = f64(w).T @ sum(x[:, t * V : (t + 1) * V] for t in range(D))
    return y * f64(c)

@@ -1,0 +1,48 @@
+import concourse.mybir as mybir
+
+BF16, F32, U16 = mybir.dt.bfloat16, mybir.dt.float32, mybir.dt.uint16
+MULT = mybir.AluOpType.mult
+
+P = 128
+M = 512
+NODES = 512
+V = 96
+PIECES = 2
+LIST_COLUMNS = PIECES * V // 16
+PIECE_COLUMNS = V // 16
+BLOCKS = M // P
+
+FLOPS = 2 * P * M * PIECES * V + M * V
+
+
+def tile_gather_matmul_kernel(tc, table, w, c, offs, out):
+    nc = tc.nc
+    with (
+        tc.tile_pool(name="held", bufs=1) as held,
+        tc.psum_pool(name="psum", bufs=BLOCKS) as psum,
+    ):
+        offsets = held.tile([P, LIST_COLUMNS], U16)
+        nodes = held.tile([P, NODES], BF16)
+        weights = held.tile([P, M], BF16)
+        node_gain = held.tile([P, V], F32)
+        result = held.tile([P, BLOCKS, V], F32)
+
+        nc.sync.dma_start(offsets[:], offs)
+        nc.sync.dma_start(nodes[:], table)
+        nc.scalar.dma_start(weights[:], w)
+        nc.scalar.dma_start(node_gain[:], c.rearrange("o v -> (o v)").partition_broadcast(P))
+
+        for b in range(BLOCKS):
+            projected = psum.tile([P, V], F32)
+            for t in range(PIECES):
+                neighbours = nodes[:].indirect(offsets[:, t * PIECE_COLUMNS : (t + 1) * PIECE_COLUMNS])
+                nc.tensor.matmul(
+                    projected[:],
+                    weights[:, b * P : (b + 1) * P],
+                    neighbours,
+                    start=t == 0,
+                    stop=t == PIECES - 1,
+                )
+            nc.vector.tensor_tensor(result[:, b, :], projected[:], node_gain[:], MULT)
+
+        nc.sync.dma_start(out.rearrange("(b p) v -> p b v", p=P), result[:])

@@ -38,11 +38,11 @@ def tile_gather_matmul_kernel(tc, table, w, c, offs, out):
                 neighbours = nodes[:].indirect(offsets[:, t * PIECE_COLUMNS : (t + 1) * PIECE_COLUMNS])
                 nc.tensor.matmul(
                     projected[:],
-                    weights[:, b * P : (b + 1) * P],
+                    weights[:, b::BLOCKS],
                     neighbours,
                     start=t == 0,
                     stop=t == PIECES - 1,
                 )
             nc.vector.tensor_tensor(result[:, b, :], projected[:], node_gain[:], MULT)
 
-        nc.sync.dma_start(out.rearrange("(b p) v -> p b v", p=P), result[:])
+        nc.sync.dma_start(out.rearrange("(p b) v -> p b v", p=P), result[:])

import concourse.mybir as mybir

BF16, F32, U16 = mybir.dt.bfloat16, mybir.dt.float32, mybir.dt.uint16
MULT = mybir.AluOpType.mult

P = 128
M = 512
NODES = 512
V = 96
PIECES = 2
LIST_COLUMNS = PIECES * V // 16
PIECE_COLUMNS = V // 16
BLOCKS = M // P

FLOPS = 2 * P * M * PIECES * V + M * V


def tile_gather_matmul_kernel(tc, table, w, c, offs, out):
    nc = tc.nc
    with (
        tc.tile_pool(name="held", bufs=1) as held,
        tc.psum_pool(name="psum", bufs=BLOCKS) as psum,
    ):
        offsets = held.tile([P, LIST_COLUMNS], U16)
        nodes = held.tile([P, NODES], BF16)
        weights = held.tile([P, M], BF16)
        node_gain = held.tile([P, V], F32)
        result = held.tile([P, BLOCKS, V], F32)

        nc.sync.dma_start(offsets[:], offs)
        nc.sync.dma_start(nodes[:], table)
        nc.scalar.dma_start(weights[:], w)
        nc.scalar.dma_start(node_gain[:], c.rearrange("o v -> (o v)").partition_broadcast(P))

        for b in range(BLOCKS):
            projected = psum.tile([P, V], F32)
            for t in range(PIECES):
                neighbours = nodes[:].indirect(offsets[:, t * PIECE_COLUMNS : (t + 1) * PIECE_COLUMNS])
                nc.tensor.matmul(
                    projected[:],
                    weights[:, b::BLOCKS],
                    neighbours,
                    start=t == 0,
                    stop=t == PIECES - 1,
                )
            nc.vector.tensor_tensor(result[:, b, :], projected[:], node_gain[:], MULT)

        nc.sync.dma_start(out.rearrange("(p b) v -> p b v", p=P), result[:])
